import numpy as np
import ml_dtypes


def mxq(x, axis, fmt="e4m3"):
    dtype, down = {"e4m3": (ml_dtypes.float8_e4m3fn, 7), "e5m2": (ml_dtypes.float8_e5m2, 14)}[fmt]
    v = np.moveaxis(np.asarray(x, np.float32).astype(ml_dtypes.bfloat16).astype(np.float64), axis, -1)
    blocks = v.reshape(v.shape[:-1] + (-1, 32))
    amax = np.abs(blocks).max(-1, keepdims=True)
    byte = np.maximum(np.where(amax > 0, np.frexp(amax)[1] - 1 + 127, 0) - down, 1)
    scale = np.exp2(byte - 127.0)
    codes = (blocks / scale).astype(np.float32).astype(dtype).astype(np.float64)
    return np.moveaxis((codes * scale).reshape(v.shape), -1, axis)


WIDE = False


def mx_kscale(k):
    if not WIDE:
        return np.ones(k)
    levels = np.array([10, -10, 5, -5, 0])
    if k % 512:
        return np.exp2(np.random.permutation(np.resize(levels, k // 32))).repeat(32)
    a = np.empty((k // 512, 16))
    for p in range(k // 512):
        a[p, :8] = np.random.permutation(np.resize(levels, 8))
        for g in range(8):
            far = levels[np.abs(levels - a[p, g]) >= 10]
            a[p, g + 8] = far[np.random.randint(len(far))]
    return np.exp2(a.ravel()).repeat(32)


def f64(x):
    return np.asarray(x).astype(np.float64)


def striped(idx):
    return np.tile(idx.reshape(-1, 16).T, (8, 1)).astype(np.uint16)


def unstriped(offs):
    return offs[:16].T.reshape(-1).astype(np.int64)


def striped8(idx):
    return np.concatenate([x.reshape(-1, 16).T for x in idx]).astype(np.uint16)


def runs(offs, k):
    lists = np.stack([offs[16 * r : 16 * r + 16].T.reshape(-1) for r in range(8)]).astype(np.int64)
    return lists[np.arange(k) % 512 // 64]


def pack_weight(w):
    k, n = w.shape
    w = f64(np.asarray(w, np.float32).astype(ml_dtypes.bfloat16)).reshape(k // 32, 32, n)
    amax = np.abs(w).max(1)
    byte = np.clip(np.where(amax > 0, np.frexp(amax)[1] - 1 + 127 - 7, 1), 1, 254)
    scaled = (w * np.exp2(127.0 - byte)[:, None, :]).reshape(k, n).astype(np.float32)
    words = np.ascontiguousarray(scaled.reshape(k // 512, 128, 4, n).transpose(0, 1, 3, 2)).astype(ml_dtypes.float8_e4m3fn).view(np.uint8)
    return words, np.ascontiguousarray(byte.astype(np.uint8).reshape(k // 512, 16, n))


def unpack_weight(words, scales):
    g, p, n, _ = words.shape
    vals = np.ascontiguousarray(words).view(ml_dtypes.float8_e4m3fn).astype(np.float64) * np.repeat(np.exp2(scales.astype(np.float64) - 127.0), 8, axis=1)[..., None]
    return vals.transpose(0, 1, 3, 2).reshape(g * 512, n)


def sigmoid(v):
    return 1.0 / (1.0 + np.exp(-np.maximum(v, -700.0)))


K, T, S, N, H, W, G = 512, 2048, 512, 512, 512, 384, 2048


def setup_inputs():
    n = np.random.standard_normal
    s = mx_kscale(K)[:, None]
    u = mx_kscale(S)
    packed_xT = pack_weight(n((K, T)) * s)
    packed_dT = pack_weight(n((K, G)) / s)
    return {
        "x_words": packed_xT[0],
        "x_scales": packed_xT[1],
        "w1": (n((K, H)) / np.sqrt(K) / s).astype(np.float32),
        "gn": (np.random.uniform(0.5, 1.5, (H, 1)) * u[:, None]).astype(np.float32),
        "w2": (n((H, N)) / np.sqrt(H) / u[:, None]).astype(np.float32),
        "d_words": packed_dT[0],
        "d_scales": packed_dT[1],
        "offs": striped(np.random.permutation(T)[:S]),
        "n1": striped(np.random.permutation(S)[:W]),
        "n2": striped(np.random.permutation(S)[:W]),
        "two": striped(np.random.permutation(T)[:S]),
        "k1": striped8(np.random.randint(0, G, (8, H))),
        "n3": striped(np.random.permutation(S)),
        "n4": striped(np.random.permutation(S)),
    }


def reference(x_words, x_scales, w1, gn, w2, d_words, d_scales, offs, n1, n2, two, k1, n3, n4):
    xq = unpack_weight(x_words, x_scales)[:, unstriped(offs)]
    y = mxq(f64(w1), 0, "e4m3").T @ xq
    old = y[:, unstriped(n1)]
    pa = y[:, unstriped(n2)]
    ra = old * sigmoid(pa)
    ds = y.copy()
    ds[:, unstriped(n1)] = ra
    z = f64(gn) * ds
    a = mxq(f64(w2), 0, "e4m3").T @ mxq(z, 0, "e4m3")
    d_k1 = unpack_weight(d_words, d_scales)[np.arange(K)[:, None], runs(k1, K)]
    x_two = unpack_weight(x_words, x_scales)[:, unstriped(two)]
    b = 0.0625 * (d_k1.T @ x_two)
    return a * (np.tanh(b[:, unstriped(n3)] - b[:, unstriped(n4)]))

@@ -1,0 +1,172 @@
+from contextlib import ExitStack
+
+import concourse.mybir as mybir
+
+K, T, S, N, H, W, G = 512, 2048, 512, 512, 512, 384, 2048
+FLOPS = 3 * 2 * 512 * 512 * 512
+
+F32 = mybir.dt.float32
+BF16 = mybir.dt.bfloat16
+I32 = mybir.dt.int32
+U32 = mybir.dt.uint32
+U16 = mybir.dt.uint16
+U8 = mybir.dt.uint8
+FP8X4 = mybir.dt.float8_e4m3fn_x4
+ACT = mybir.ActivationFunctionType
+ALU = mybir.AluOpType
+
+P = 128
+PACK = 4
+Y_WINDOW = 2 * W
+B_WINDOW = 2 * S
+
+
+def tile_picked_cdjoinjointbkgate_none_p_kernel(
+    tc, x_words, x_scales, w1, gn, w2, d_words, d_scales, offs, n1, n2, two, k1, n3, n4, out
+):
+    nc = tc.nc
+    with ExitStack() as ctx:
+        sb = ctx.enter_context(tc.tile_pool(name="sb", bufs=1))
+        ps = ctx.enter_context(tc.psum_pool(name="ps", bufs=1))
+
+        def load_list(src, name):
+            t = sb.tile(list(src.shape), U16, name=name)
+            nc.sync.dma_start(t[:], src)
+            return t
+
+        def new(shape, dtype, name):
+            return sb.tile(shape, dtype, name=name, align_bytes=64)
+
+        x_sc = new([P, T], U8, "x_sc")
+        d_sc = new([P, G], U8, "d_sc")
+        dk_plane = new([P, H], U8, "dk_plane")
+        y_win = [new([P, Y_WINDOW], F32, f"y_win{t}") for t in range(PACK)]
+        b_win = [new([P, B_WINDOW], F32, f"b_win{t}") for t in range(PACK)]
+        nc.gpsimd.memset(x_sc[:].bitcast(I32), 0)
+        nc.vector.memset(d_sc[:].bitcast(I32), 0)
+        nc.gpsimd.memset(dk_plane[:].bitcast(I32), 0)
+        for t in range(PACK):
+            nc.vector.memset(y_win[t][:, S:], 0.0)
+        for t in range(PACK):
+            nc.vector.memset(b_win[t][:, S:], 0.0)
+
+        offs_sb = load_list(offs, "offs_sb")
+        two_sb = load_list(two, "two_sb")
+        for q in range(4):
+            nc.sync.dma_start(x_sc[32 * q : 32 * q + 4, :].bitcast(I32), x_scales[0, 4 * q : 4 * q + 4, :].bitcast(I32))
+        HALF = H // 2
+        w1_rows = w1.rearrange("(p j) c -> p j c", j=PACK)
+        w1_raw = [new([P, PACK, HALF], F32, f"w1_raw{h}") for h in range(2)]
+        for h in range(2):
+            nc.sync.dma_start(w1_raw[h][:], w1_rows[:, :, h * HALF : (h + 1) * HALF])
+        k1_sb = load_list(k1, "k1_sb")
+        for e in range(2):
+            nc.sync.dma_start(d_sc[e:P:16, :].bitcast(I32), d_scales[0, e:16:2, :].bitcast(I32))
+        x_w = new([P, T], U32, "x_w")
+        nc.sync.dma_start(x_w[:].bitcast(I32), x_words[0].rearrange("p n r -> p (n r)").bitcast(I32))
+        n2_sb = load_list(n2, "n2_sb")
+        n1_sb = load_list(n1, "n1_sb")
+        d_w = new([P, G], U32, "d_w")
+        nc.sync.dma_start(d_w[:].bitcast(I32), d_words[0].rearrange("p n r -> p (n r)").bitcast(I32))
+        gn_sb = new([P, PACK], F32, "gn_sb")
+        nc.sync.dma_start(gn_sb[:], gn.rearrange("(p t) o -> p (t o)", t=PACK))
+        w2_raw = new([P, PACK, N], F32, "w2_raw")
+        nc.sync.dma_start(w2_raw[:], w2.rearrange("(p j) c -> p j c", j=PACK))
+        n3_sb = load_list(n3, "n3_sb")
+        n4_sb = load_list(n4, "n4_sb")
+
+        w1_bf = new([P, PACK, P, PACK], BF16, "w1_bf")
+        for h in range(2):
+            nc.scalar.copy(
+                w1_bf[:, :, h * 64 : (h + 1) * 64, :].rearrange("p t m j -> p m j t"),
+                w1_raw[h][:].rearrange("p j (m t) -> p m j t", t=PACK),
+            )
+        xo_w = new([P, S], U32, "xo_w")
+        xo_s = new([P, S], U8, "xo_s")
+        xt_w = new([P, S], U32, "xt_w")
+        xt_s = new([P, S], U8, "xt_s")
+        nc.vector.tensor_copy(xo_s[:], x_sc[:].indirect(offs_sb[:]))
+        nc.vector.tensor_copy(xo_w[:], x_w[:].indirect(offs_sb[:]))
+        w1_q = new([P, H], U32, "w1_q")
+        w1_s = new([P, H], U8, "w1_s")
+        nc.vector.quantize_mx(w1_q[:].bitcast(FP8X4), w1_s[:], w1_bf[:].rearrange("p t m j -> p (t m j)"))
+        y_ps = []
+        for t in range(PACK):
+            cols = slice(t * P, (t + 1) * P)
+            acc = ps.tile([P, S], F32, name=f"y_ps{t}", tag=f"bank{t}")
+            nc.tensor.matmul_mx(acc[:], w1_q[:, cols].bitcast(FP8X4), w1_s[:, cols], xo_w[:].bitcast(FP8X4), xo_s[:], start=True, stop=True)
+            y_ps.append(acc)
+
+        nc.vector.tensor_copy(xt_s[:], x_sc[:].indirect(two_sb[:]))
+        nc.vector.tensor_copy(xt_w[:], x_w[:].indirect(two_sb[:]))
+        dk_w = new([P, H], U32, "dk_w")
+        dk_s = new([P, H], U8, "dk_s")
+        nc.vector.tensor_copy(dk_s[:], d_sc[:].indirect(k1_sb[:]))
+        for r in range(4):
+            nc.sync.dma_start(dk_plane[r:P:32, :].bitcast(I32), dk_s[16 * (r // 2) + r % 2 : P : 32, :].bitcast(I32))
+        nc.vector.tensor_copy(dk_w[:], d_w[:].indirect(k1_sb[:]))
+
+        b_ps = []
+        for t in range(PACK):
+            cols = slice(t * P, (t + 1) * P)
+            acc = ps.tile([P, S], F32, name=f"b_ps{t}", tag=f"bank{PACK + t}")
+            nc.tensor.matmul_mx(acc[:], dk_w[:, cols].bitcast(FP8X4), dk_plane[:, cols], xt_w[:].bitcast(FP8X4), xt_s[:], start=True, stop=True)
+            b_ps.append(acc)
+
+        z_rows = new([P, PACK, S], BF16, "z_rows")
+        sig = [new([P, W], F32, f"sig{t}") for t in range(PACK)]
+        old = [new([P, W], F32, f"old{t}") for t in range(PACK)]
+        for t in range(PACK):
+            nc.scalar.copy(y_win[t][:, :S], y_ps[t][:])
+            nc.scalar.activation(sig[t][:], y_win[t][:].indirect(n2_sb[:]), ACT.Sigmoid)
+            if t < 2:
+                nc.vector.tensor_tensor(old[t][:], y_win[t][:].indirect(n1_sb[:]), sig[t][:], ALU.mult)
+            else:
+                nc.vector.tensor_copy(old[t][:], y_win[t][:].indirect(n1_sb[:]))
+                nc.vector.tensor_tensor(y_win[t][:].indirect(n1_sb[:]), old[t][:], sig[t][:], ALU.mult)
+        for t in range(2):
+            nc.scalar.activation(y_win[t][:].indirect(n1_sb[:]), old[t][:], ACT.Copy)
+        for t in (2, 0, 3, 1):
+            nc.vector.tensor_scalar(z_rows[:, t, :], y_win[t][:, :S], gn_sb[:, t : t + 1], None, ALU.mult)
+
+        z_bf = new([P, S, PACK], BF16, "z_bf")
+        nc.vector.tensor_copy(
+            z_bf[:].rearrange("p (c i) t -> p c t i", i=4), z_rows[:].rearrange("p t (c i) -> p c t i", i=4)
+        )
+        z_q = new([P, S], U32, "z_q")
+        z_s = new([P, S], U8, "z_s")
+        nc.vector.quantize_mx(z_q[:].bitcast(FP8X4), z_s[:], z_bf[:].rearrange("p c t -> p (c t)"))
+
+        w2_bf = new([P, N, PACK], BF16, "w2_bf")
+        nc.scalar.copy(
+            w2_bf[:].rearrange("p (c i) j -> p c j i", i=4), w2_raw[:].rearrange("p j (c i) -> p c j i", i=4)
+        )
+        w2_q = new([P, N], U32, "w2_q")
+        w2_s = new([P, N], U8, "w2_s")
+        nc.vector.quantize_mx(w2_q[:].bitcast(FP8X4), w2_s[:], w2_bf[:].rearrange("p c j -> p (c j)"))
+
+        a_ps = []
+        for t in range(PACK):
+            cols = slice(t * P, (t + 1) * P)
+            acc = ps.tile([P, S], F32, name=f"a_ps{t}", tag=f"bank{t}")
+            nc.tensor.matmul_mx(acc[:], w2_q[:, cols].bitcast(FP8X4), w2_s[:, cols], z_q[:].bitcast(FP8X4), z_s[:], start=True, stop=True)
+            a_ps.append(acc)
+        diff = [new([P, S], F32, f"diff{t}") for t in range(PACK)]
+
+        def look_up(t):
+            b4 = new([P, S], F32, f"b4_{t}")
+            nc.scalar.copy(b_win[t][:, :S], b_ps[t][:])
+            nc.scalar.activation(b4[:], b_win[t][:].indirect(n4_sb[:]), ACT.Copy)
+            nc.vector.tensor_tensor(diff[t][:], b_win[t][:].indirect(n3_sb[:]), b4[:], ALU.subtract)
+
+        def finish(t):
+            gate = new([P, S], F32, f"gate{t}")
+            res = new([P, S], F32, f"res{t}")
+            nc.scalar.activation(gate[:], diff[t][:], ACT.Tanh, scale=0.0625)
+            nc.vector.tensor_tensor(res[:], a_ps[t][:], gate[:], ALU.mult)
+            nc.sync.dma_start(out[t * P : (t + 1) * P, :], res[:])
+
+        for t in range(PACK):
+            look_up(t)
+        for t in range(PACK):
+            finish(t)

@@ -19,6 +19,7 @@ P = 128
 PACK = 4
 Y_WINDOW = 2 * W
 B_WINDOW = 2 * S
+W1_FIRST = 384
 
 
 def tile_picked_cdjoinjointbkgate_none_p_kernel(
@@ -34,8 +35,8 @@ def tile_picked_cdjoinjointbkgate_none_p_kernel(
             nc.sync.dma_start(t[:], src)
             return t
 
-        def new(shape, dtype, name):
-            return sb.tile(shape, dtype, name=name, align_bytes=64)
+        def new(shape, dtype, name, tag=""):
+            return sb.tile(shape, dtype, name=name, tag=tag or name, align_bytes=64)
 
         x_sc = new([P, T], U8, "x_sc")
         d_sc = new([P, G], U8, "d_sc")
@@ -50,40 +51,41 @@ def tile_picked_cdjoinjointbkgate_none_p_kernel(
         for t in range(PACK):
             nc.vector.memset(b_win[t][:, S:], 0.0)
 
+        warm = new([P, 1], F32, "warm")
+        nc.scalar.activation(warm[:], y_win[0][:, S : S + 1], ACT.Sigmoid)
         offs_sb = load_list(offs, "offs_sb")
         two_sb = load_list(two, "two_sb")
+        w1_rows = w1.rearrange("(p j) c -> p j c", j=PACK)
+        w1_parts = [(0, W1_FIRST), (W1_FIRST, H)]
+        w1_raw = [new([P, PACK, hi - lo], F32, f"w1_raw{lo}") for lo, hi in w1_parts]
+        nc.sync.dma_start(w1_raw[0][:], w1_rows[:, :, :W1_FIRST])
         for q in range(4):
             nc.sync.dma_start(x_sc[32 * q : 32 * q + 4, :].bitcast(I32), x_scales[0, 4 * q : 4 * q + 4, :].bitcast(I32))
-        HALF = H // 2
-        w1_rows = w1.rearrange("(p j) c -> p j c", j=PACK)
-        w1_raw = [new([P, PACK, HALF], F32, f"w1_raw{h}") for h in range(2)]
-        for h in range(2):
-            nc.sync.dma_start(w1_raw[h][:], w1_rows[:, :, h * HALF : (h + 1) * HALF])
+        x_w = new([P, T], U32, "x_w")
+        nc.sync.dma_start(x_w[:].bitcast(I32), x_words[0].rearrange("p n r -> p (n r)").bitcast(I32))
+        nc.sync.dma_start(w1_raw[1][:], w1_rows[:, :, W1_FIRST:])
+        n2_sb = load_list(n2, "n2_sb")
+        n1_sb = load_list(n1, "n1_sb")
         k1_sb = load_list(k1, "k1_sb")
         for e in range(2):
             nc.sync.dma_start(d_sc[e:P:16, :].bitcast(I32), d_scales[0, e:16:2, :].bitcast(I32))
-        x_w = new([P, T], U32, "x_w")
-        nc.sync.dma_start(x_w[:].bitcast(I32), x_words[0].rearrange("p n r -> p (n r)").bitcast(I32))
-        n2_sb = load_list(n2, "n2_sb")
-        n1_sb = load_list(n1, "n1_sb")
         d_w = new([P, G], U32, "d_w")
         nc.sync.dma_start(d_w[:].bitcast(I32), d_words[0].rearrange("p n r -> p (n r)").bitcast(I32))
-        gn_sb = new([P, PACK], F32, "gn_sb")
-        nc.sync.dma_start(gn_sb[:], gn.rearrange("(p t) o -> p (t o)", t=PACK))
         w2_raw = new([P, PACK, N], F32, "w2_raw")
         nc.sync.dma_start(w2_raw[:], w2.rearrange("(p j) c -> p j c", j=PACK))
-        n3_sb = load_list(n3, "n3_sb")
+        gn_sb = new([P, PACK], F32, "gn_sb")
+        nc.sync.dma_start(gn_sb[:], gn.rearrange("(p t) o -> p (t o)", t=PACK))
         n4_sb = load_list(n4, "n4_sb")
+        n3_sb = load_list(n3, "n3_sb")
 
         w1_bf = new([P, PACK, P, PACK], BF16, "w1_bf")
-        for h in range(2):
+        for raw, (lo, hi) in zip(w1_raw, w1_parts):
             nc.scalar.copy(
-                w1_bf[:, :, h * 64 : (h + 1) * 64, :].rearrange("p t m j -> p m j t"),
-                w1_raw[h][:].rearrange("p j (m t) -> p m j t", t=PACK),
+                w1_bf[:, :, lo // PACK : hi // PACK, :].rearrange("p t m j -> p m j t"),
+                raw[:].rearrange("p j (m t) -> p m j t", t=PACK),
             )
         xo_w = new([P, S], U32, "xo_w")
         xo_s = new([P, S], U8, "xo_s")
-        xt_w = new([P, S], U32, "xt_w")
         xt_s = new([P, S], U8, "xt_s")
         nc.vector.tensor_copy(xo_s[:], x_sc[:].indirect(offs_sb[:]))
         nc.vector.tensor_copy(xo_w[:], x_w[:].indirect(offs_sb[:]))
@@ -98,6 +100,7 @@ def tile_picked_cdjoinjointbkgate_none_p_kernel(
             y_ps.append(acc)
 
         nc.vector.tensor_copy(xt_s[:], x_sc[:].indirect(two_sb[:]))
+        xt_w = new([P, S], U32, "xt_w", tag="w1_bf")
         nc.vector.tensor_copy(xt_w[:], x_w[:].indirect(two_sb[:]))
         dk_w = new([P, H], U32, "dk_w")
         dk_s = new([P, H], U8, "dk_s")
@@ -151,18 +154,18 @@ def tile_picked_cdjoinjointbkgate_none_p_kernel(
             acc = ps.tile([P, S], F32, name=f"a_ps{t}", tag=f"bank{t}")
             nc.tensor.matmul_mx(acc[:], w2_q[:, cols].bitcast(FP8X4), w2_s[:, cols], z_q[:].bitcast(FP8X4), z_s[:], start=True, stop=True)
             a_ps.append(acc)
-        diff = [new([P, S], F32, f"diff{t}") for t in range(PACK)]
+        b4 = new([P, PACK, S], F32, "b4", tag="w2_raw")
+        diff = new([P, PACK, S], F32, "diff", tag="z_bf")
 
         def look_up(t):
-            b4 = new([P, S], F32, f"b4_{t}")
             nc.scalar.copy(b_win[t][:, :S], b_ps[t][:])
-            nc.scalar.activation(b4[:], b_win[t][:].indirect(n4_sb[:]), ACT.Copy)
-            nc.vector.tensor_tensor(diff[t][:], b_win[t][:].indirect(n3_sb[:]), b4[:], ALU.subtract)
+            nc.scalar.activation(b4[:, t, :], b_win[t][:].indirect(n4_sb[:]), ACT.Copy)
+            nc.vector.tensor_tensor(diff[:, t, :], b_win[t][:].indirect(n3_sb[:]), b4[:, t, :], ALU.subtract)
 
         def finish(t):
             gate = new([P, S], F32, f"gate{t}")
             res = new([P, S], F32, f"res{t}")
-            nc.scalar.activation(gate[:], diff[t][:], ACT.Tanh, scale=0.0625)
+            nc.scalar.activation(gate[:], diff[:, t, :], ACT.Tanh, scale=0.0625)
             nc.vector.tensor_tensor(res[:], a_ps[t][:], gate[:], ALU.mult)
             nc.sync.dma_start(out[t * P : (t + 1) * P, :], res[:])
 

@@ -20,6 +20,7 @@ PACK = 4
 Y_WINDOW = 2 * W
 B_WINDOW = 2 * S
 W1_FIRST = 384
+W2_FIRST = 192
 
 
 def tile_picked_cdjoinjointbkgate_none_p_kernel(
@@ -54,25 +55,28 @@ def tile_picked_cdjoinjointbkgate_none_p_kernel(
         warm = new([P, 1], F32, "warm")
         nc.scalar.activation(warm[:], y_win[0][:, S : S + 1], ACT.Sigmoid)
         offs_sb = load_list(offs, "offs_sb")
-        two_sb = load_list(two, "two_sb")
         w1_rows = w1.rearrange("(p j) c -> p j c", j=PACK)
         w1_parts = [(0, W1_FIRST), (W1_FIRST, H)]
         w1_raw = [new([P, PACK, hi - lo], F32, f"w1_raw{lo}") for lo, hi in w1_parts]
         nc.sync.dma_start(w1_raw[0][:], w1_rows[:, :, :W1_FIRST])
+        two_sb = load_list(two, "two_sb")
         for q in range(4):
             nc.sync.dma_start(x_sc[32 * q : 32 * q + 4, :].bitcast(I32), x_scales[0, 4 * q : 4 * q + 4, :].bitcast(I32))
         x_w = new([P, T], U32, "x_w")
         nc.sync.dma_start(x_w[:].bitcast(I32), x_words[0].rearrange("p n r -> p (n r)").bitcast(I32))
         nc.sync.dma_start(w1_raw[1][:], w1_rows[:, :, W1_FIRST:])
+        w2_rows = w2.rearrange("(p j) c -> p j c", j=PACK)
+        w2_parts = [(0, W2_FIRST), (W2_FIRST, N)]
+        w2_raw = [new([P, PACK, hi - lo], F32, f"w2_raw{lo}") for lo, hi in w2_parts]
+        nc.sync.dma_start(w2_raw[0][:], w2_rows[:, :, :W2_FIRST])
         n2_sb = load_list(n2, "n2_sb")
-        n1_sb = load_list(n1, "n1_sb")
         k1_sb = load_list(k1, "k1_sb")
         for e in range(2):
             nc.sync.dma_start(d_sc[e:P:16, :].bitcast(I32), d_scales[0, e:16:2, :].bitcast(I32))
         d_w = new([P, G], U32, "d_w")
         nc.sync.dma_start(d_w[:].bitcast(I32), d_words[0].rearrange("p n r -> p (n r)").bitcast(I32))
-        w2_raw = new([P, PACK, N], F32, "w2_raw")
-        nc.sync.dma_start(w2_raw[:], w2.rearrange("(p j) c -> p j c", j=PACK))
+        n1_sb = load_list(n1, "n1_sb")
+        nc.sync.dma_start(w2_raw[1][:], w2_rows[:, :, W2_FIRST:])
         gn_sb = new([P, PACK], F32, "gn_sb")
         nc.sync.dma_start(gn_sb[:], gn.rearrange("(p t) o -> p (t o)", t=PACK))
         n4_sb = load_list(n4, "n4_sb")
@@ -141,9 +145,10 @@ def tile_picked_cdjoinjointbkgate_none_p_kernel(
         nc.vector.quantize_mx(z_q[:].bitcast(FP8X4), z_s[:], z_bf[:].rearrange("p c t -> p (c t)"))
 
         w2_bf = new([P, N, PACK], BF16, "w2_bf")
-        nc.scalar.copy(
-            w2_bf[:].rearrange("p (c i) j -> p c j i", i=4), w2_raw[:].rearrange("p j (c i) -> p c j i", i=4)
-        )
+        for raw, (lo, hi) in zip(w2_raw, w2_parts):
+            nc.scalar.copy(
+                w2_bf[:, lo:hi, :].rearrange("p (c i) j -> p c j i", i=4), raw[:].rearrange("p j (c i) -> p c j i", i=4)
+            )
         w2_q = new([P, N], U32, "w2_q")
         w2_s = new([P, N], U8, "w2_s")
         nc.vector.quantize_mx(w2_q[:].bitcast(FP8X4), w2_s[:], w2_bf[:].rearrange("p c j -> p (c j)"))
@@ -154,7 +159,7 @@ def tile_picked_cdjoinjointbkgate_none_p_kernel(
             acc = ps.tile([P, S], F32, name=f"a_ps{t}", tag=f"bank{t}")
             nc.tensor.matmul_mx(acc[:], w2_q[:, cols].bitcast(FP8X4), w2_s[:, cols], z_q[:].bitcast(FP8X4), z_s[:], start=True, stop=True)
             a_ps.append(acc)
-        b4 = new([P, PACK, S], F32, "b4", tag="w2_raw")
+        b4 = new([P, PACK, S], F32, "b4", tag=f"w2_raw{W2_FIRST}")
         diff = new([P, PACK, S], F32, "diff", tag="z_bf")
 
         def look_up(t):

from contextlib import ExitStack

import concourse.mybir as mybir

K, T, S, N, H, W, G = 512, 2048, 512, 512, 512, 384, 2048
FLOPS = 3 * 2 * 512 * 512 * 512

F32 = mybir.dt.float32
BF16 = mybir.dt.bfloat16
I32 = mybir.dt.int32
U32 = mybir.dt.uint32
U16 = mybir.dt.uint16
U8 = mybir.dt.uint8
FP8X4 = mybir.dt.float8_e4m3fn_x4
ACT = mybir.ActivationFunctionType
ALU = mybir.AluOpType

P = 128
PACK = 4
Y_WINDOW = 2 * W
B_WINDOW = 2 * S
W1_FIRST = 384
W2_FIRST = 192


def tile_picked_cdjoinjointbkgate_none_p_kernel(
    tc, x_words, x_scales, w1, gn, w2, d_words, d_scales, offs, n1, n2, two, k1, n3, n4, out
):
    nc = tc.nc
    with ExitStack() as ctx:
        sb = ctx.enter_context(tc.tile_pool(name="sb", bufs=1))
        ps = ctx.enter_context(tc.psum_pool(name="ps", bufs=1))

        def load_list(src, name):
            t = sb.tile(list(src.shape), U16, name=name)
            nc.sync.dma_start(t[:], src)
            return t

        def new(shape, dtype, name, tag=""):
            return sb.tile(shape, dtype, name=name, tag=tag or name, align_bytes=64)

        x_sc = new([P, T], U8, "x_sc")
        d_sc = new([P, G], U8, "d_sc")
        dk_plane = new([P, H], U8, "dk_plane")
        y_win = [new([P, Y_WINDOW], F32, f"y_win{t}") for t in range(PACK)]
        b_win = [new([P, B_WINDOW], F32, f"b_win{t}") for t in range(PACK)]
        nc.gpsimd.memset(x_sc[:].bitcast(I32), 0)
        nc.vector.memset(d_sc[:].bitcast(I32), 0)
        nc.gpsimd.memset(dk_plane[:].bitcast(I32), 0)
        for t in range(PACK):
            nc.vector.memset(y_win[t][:, S:], 0.0)
        for t in range(PACK):
            nc.vector.memset(b_win[t][:, S:], 0.0)

        warm = new([P, 1], F32, "warm")
        nc.scalar.activation(warm[:], y_win[0][:, S : S + 1], ACT.Sigmoid)
        offs_sb = load_list(offs, "offs_sb")
        w1_rows = w1.rearrange("(p j) c -> p j c", j=PACK)
        w1_parts = [(0, W1_FIRST), (W1_FIRST, H)]
        w1_raw = [new([P, PACK, hi - lo], F32, f"w1_raw{lo}") for lo, hi in w1_parts]
        nc.sync.dma_start(w1_raw[0][:], w1_rows[:, :, :W1_FIRST])
        two_sb = load_list(two, "two_sb")
        for q in range(4):
            nc.sync.dma_start(x_sc[32 * q : 32 * q + 4, :].bitcast(I32), x_scales[0, 4 * q : 4 * q + 4, :].bitcast(I32))
        x_w = new([P, T], U32, "x_w")
        nc.sync.dma_start(x_w[:].bitcast(I32), x_words[0].rearrange("p n r -> p (n r)").bitcast(I32))
        nc.sync.dma_start(w1_raw[1][:], w1_rows[:, :, W1_FIRST:])
        w2_rows = w2.rearrange("(p j) c -> p j c", j=PACK)
        w2_parts = [(0, W2_FIRST), (W2_FIRST, N)]
        w2_raw = [new([P, PACK, hi - lo], F32, f"w2_raw{lo}") for lo, hi in w2_parts]
        nc.sync.dma_start(w2_raw[0][:], w2_rows[:, :, :W2_FIRST])
        n2_sb = load_list(n2, "n2_sb")
        k1_sb = load_list(k1, "k1_sb")
        for e in range(2):
            nc.sync.dma_start(d_sc[e:P:16, :].bitcast(I32), d_scales[0, e:16:2, :].bitcast(I32))
        d_w = new([P, G], U32, "d_w")
        nc.sync.dma_start(d_w[:].bitcast(I32), d_words[0].rearrange("p n r -> p (n r)").bitcast(I32))
        n1_sb = load_list(n1, "n1_sb")
        nc.sync.dma_start(w2_raw[1][:], w2_rows[:, :, W2_FIRST:])
        gn_sb = new([P, PACK], F32, "gn_sb")
        nc.sync.dma_start(gn_sb[:], gn.rearrange("(p t) o -> p (t o)", t=PACK))
        n4_sb = load_list(n4, "n4_sb")
        n3_sb = load_list(n3, "n3_sb")

        w1_bf = new([P, PACK, P, PACK], BF16, "w1_bf")
        for raw, (lo, hi) in zip(w1_raw, w1_parts):
            nc.scalar.copy(
                w1_bf[:, :, lo // PACK : hi // PACK, :].rearrange("p t m j -> p m j t"),
                raw[:].rearrange("p j (m t) -> p m j t", t=PACK),
            )
        xo_w = new([P, S], U32, "xo_w")
        xo_s = new([P, S], U8, "xo_s")
        xt_s = new([P, S], U8, "xt_s")
        nc.vector.tensor_copy(xo_s[:], x_sc[:].indirect(offs_sb[:]))
        nc.vector.tensor_copy(xo_w[:], x_w[:].indirect(offs_sb[:]))
        w1_q = new([P, H], U32, "w1_q")
        w1_s = new([P, H], U8, "w1_s")
        nc.vector.quantize_mx(w1_q[:].bitcast(FP8X4), w1_s[:], w1_bf[:].rearrange("p t m j -> p (t m j)"))
        y_ps = []
        for t in range(PACK):
            cols = slice(t * P, (t + 1) * P)
            acc = ps.tile([P, S], F32, name=f"y_ps{t}", tag=f"bank{t}")
            nc.tensor.matmul_mx(acc[:], w1_q[:, cols].bitcast(FP8X4), w1_s[:, cols], xo_w[:].bitcast(FP8X4), xo_s[:], start=True, stop=True)
            y_ps.append(acc)

        nc.vector.tensor_copy(xt_s[:], x_sc[:].indirect(two_sb[:]))
        xt_w = new([P, S], U32, "xt_w", tag="w1_bf")
        nc.vector.tensor_copy(xt_w[:], x_w[:].indirect(two_sb[:]))
        dk_w = new([P, H], U32, "dk_w")
        dk_s = new([P, H], U8, "dk_s")
        nc.vector.tensor_copy(dk_s[:], d_sc[:].indirect(k1_sb[:]))
        for r in range(4):
            nc.sync.dma_start(dk_plane[r:P:32, :].bitcast(I32), dk_s[16 * (r // 2) + r % 2 : P : 32, :].bitcast(I32))
        nc.vector.tensor_copy(dk_w[:], d_w[:].indirect(k1_sb[:]))

        b_ps = []
        for t in range(PACK):
            cols = slice(t * P, (t + 1) * P)
            acc = ps.tile([P, S], F32, name=f"b_ps{t}", tag=f"bank{PACK + t}")
            nc.tensor.matmul_mx(acc[:], dk_w[:, cols].bitcast(FP8X4), dk_plane[:, cols], xt_w[:].bitcast(FP8X4), xt_s[:], start=True, stop=True)
            b_ps.append(acc)

        z_rows = new([P, PACK, S], BF16, "z_rows")
        sig = [new([P, W], F32, f"sig{t}") for t in range(PACK)]
        old = [new([P, W], F32, f"old{t}") for t in range(PACK)]
        for t in range(PACK):
            nc.scalar.copy(y_win[t][:, :S], y_ps[t][:])
            nc.scalar.activation(sig[t][:], y_win[t][:].indirect(n2_sb[:]), ACT.Sigmoid)
            if t < 2:
                nc.vector.tensor_tensor(old[t][:], y_win[t][:].indirect(n1_sb[:]), sig[t][:], ALU.mult)
            else:
                nc.vector.tensor_copy(old[t][:], y_win[t][:].indirect(n1_sb[:]))
                nc.vector.tensor_tensor(y_win[t][:].indirect(n1_sb[:]), old[t][:], sig[t][:], ALU.mult)
        for t in range(2):
            nc.scalar.activation(y_win[t][:].indirect(n1_sb[:]), old[t][:], ACT.Copy)
        for t in (2, 0, 3, 1):
            nc.vector.tensor_scalar(z_rows[:, t, :], y_win[t][:, :S], gn_sb[:, t : t + 1], None, ALU.mult)

        z_bf = new([P, S, PACK], BF16, "z_bf")
        nc.vector.tensor_copy(
            z_bf[:].rearrange("p (c i) t -> p c t i", i=4), z_rows[:].rearrange("p t (c i) -> p c t i", i=4)
        )
        z_q = new([P, S], U32, "z_q")
        z_s = new([P, S], U8, "z_s")
        nc.vector.quantize_mx(z_q[:].bitcast(FP8X4), z_s[:], z_bf[:].rearrange("p c t -> p (c t)"))

        w2_bf = new([P, N, PACK], BF16, "w2_bf")
        for raw, (lo, hi) in zip(w2_raw, w2_parts):
            nc.scalar.copy(
                w2_bf[:, lo:hi, :].rearrange("p (c i) j -> p c j i", i=4), raw[:].rearrange("p j (c i) -> p c j i", i=4)
            )
        w2_q = new([P, N], U32, "w2_q")
        w2_s = new([P, N], U8, "w2_s")
        nc.vector.quantize_mx(w2_q[:].bitcast(FP8X4), w2_s[:], w2_bf[:].rearrange("p c j -> p (c j)"))

        a_ps = []
        for t in range(PACK):
            cols = slice(t * P, (t + 1) * P)
            acc = ps.tile([P, S], F32, name=f"a_ps{t}", tag=f"bank{t}")
            nc.tensor.matmul_mx(acc[:], w2_q[:, cols].bitcast(FP8X4), w2_s[:, cols], z_q[:].bitcast(FP8X4), z_s[:], start=True, stop=True)
            a_ps.append(acc)
        b4 = new([P, PACK, S], F32, "b4", tag=f"w2_raw{W2_FIRST}")
        diff = new([P, PACK, S], F32, "diff", tag="z_bf")

        def look_up(t):
            nc.scalar.copy(b_win[t][:, :S], b_ps[t][:])
            nc.scalar.activation(b4[:, t, :], b_win[t][:].indirect(n4_sb[:]), ACT.Copy)
            nc.vector.tensor_tensor(diff[:, t, :], b_win[t][:].indirect(n3_sb[:]), b4[:, t, :], ALU.subtract)

        def finish(t):
            gate = new([P, S], F32, f"gate{t}")
            res = new([P, S], F32, f"res{t}")
            nc.scalar.activation(gate[:], diff[:, t, :], ACT.Tanh, scale=0.0625)
            nc.vector.tensor_tensor(res[:], a_ps[t][:], gate[:], ALU.mult)
            nc.sync.dma_start(out[t * P : (t + 1) * P, :], res[:])

        for t in range(PACK):
            look_up(t)
        for t in range(PACK):
            finish(t)
